import numpy as np
import ml_dtypes


def mxq(x, axis, fmt="e4m3"):
    dtype, down = {"e4m3": (ml_dtypes.float8_e4m3fn, 7), "e5m2": (ml_dtypes.float8_e5m2, 14)}[fmt]
    v = np.moveaxis(np.asarray(x, np.float32).astype(ml_dtypes.bfloat16).astype(np.float64), axis, -1)
    blocks = v.reshape(v.shape[:-1] + (-1, 32))
    amax = np.abs(blocks).max(-1, keepdims=True)
    byte = np.maximum(np.where(amax > 0, np.frexp(amax)[1] - 1 + 127, 0) - down, 1)
    scale = np.exp2(byte - 127.0)
    codes = (blocks / scale).astype(np.float32).astype(dtype).astype(np.float64)
    return np.moveaxis((codes * scale).reshape(v.shape), -1, axis)


WIDE = False


def mx_kscale(k):
    if not WIDE:
        return np.ones(k)
    levels = np.array([10, -10, 5, -5, 0])
    if k % 512:
        return np.exp2(np.random.permutation(np.resize(levels, k // 32))).repeat(32)
    a = np.empty((k // 512, 16))
    for p in range(k // 512):
        a[p, :8] = np.random.permutation(np.resize(levels, 8))
        for g in range(8):
            far = levels[np.abs(levels - a[p, g]) >= 10]
            a[p, g + 8] = far[np.random.randint(len(far))]
    return np.exp2(a.ravel()).repeat(32)


def f64(x):
    return np.asarray(x).astype(np.float64)


def striped(idx):
    return np.tile(idx.reshape(-1, 16).T, (8, 1)).astype(np.uint16)


def unstriped(offs):
    return offs[:16].T.reshape(-1).astype(np.int64)


def pack_weight(w):
    k, n = w.shape
    w = f64(np.asarray(w, np.float32).astype(ml_dtypes.bfloat16)).reshape(k // 32, 32, n)
    amax = np.abs(w).max(1)
    byte = np.clip(np.where(amax > 0, np.frexp(amax)[1] - 1 + 127 - 7, 1), 1, 254)
    scaled = (w * np.exp2(127.0 - byte)[:, None, :]).reshape(k, n).astype(np.float32)
    words = np.ascontiguousarray(scaled.reshape(k // 512, 128, 4, n).transpose(0, 1, 3, 2)).astype(ml_dtypes.float8_e4m3fn).view(np.uint8)
    return words, np.ascontiguousarray(byte.astype(np.uint8).reshape(k // 512, 16, n))


def unpack_weight(words, scales):
    g, p, n, _ = words.shape
    vals = np.ascontiguousarray(words).view(ml_dtypes.float8_e4m3fn).astype(np.float64) * np.repeat(np.exp2(scales.astype(np.float64) - 127.0), 8, axis=1)[..., None]
    return vals.transpose(0, 1, 3, 2).reshape(g * 512, n)


K, T, S, N, V = 512, 1024, 512, 128, 256


def setup_inputs():
    n = np.random.standard_normal
    s = mx_kscale(K)[:, None]
    packed_xT = pack_weight(n((K, T)) * s)
    return {
        "x_words": packed_xT[0],
        "x_scales": packed_xT[1],
        "w1": (n((K, N)) / np.sqrt(K) / s).astype(np.float32),
        "w2": (n((K, N)) / np.sqrt(K) / s).astype(np.float32),
        "gx": (n((N, V))).astype(np.float32),
        "gy": (n((N, V))).astype(np.float32),
        "gt": (n((N, V))).astype(np.float32),
        "reg": (np.random.uniform(0.5, 3.0, (N, 1))).astype(np.float32),
        "offs": striped(np.random.permutation(T)[:S]),
        "pos1": striped(np.random.permutation(S)[:V]),
        "pos2": striped(np.random.permutation(S)[:V]),
        "pos3": striped(np.random.permutation(S)[:V]),
        "pos4": striped(np.random.permutation(S)[:V]),
    }


def reference(x_words, x_scales, w1, w2, gx, gy, gt, reg, offs, pos1, pos2, pos3, pos4):
    xq = unpack_weight(x_words, x_scales)[:, unstriped(offs)]
    uo = mxq(f64(w1), 0, "e4m3").T @ xq
    ub = (uo[:, unstriped(pos1)] + uo[:, unstriped(pos2)] + uo[:, unstriped(pos3)] + uo[:, unstriped(pos4)]) / 4
    vo = mxq(f64(w2), 0, "e4m3").T @ xq
    vb = (vo[:, unstriped(pos1)] + vo[:, unstriped(pos2)] + vo[:, unstriped(pos3)] + vo[:, unstriped(pos4)]) / 4
    res = f64(gx) * ub + f64(gy) * vb + f64(gt)
    rob = res / (np.sqrt((res) ** 2 + 0.2))
    nu = ub - ((f64(gx) * rob) / ((f64(gx)) ** 2 + (f64(gy)) ** 2 + f64(reg)))
    nv = vb - ((f64(gy) * rob) / ((f64(gx)) ** 2 + (f64(gy)) ** 2 + f64(reg)))
    return (nu) ** 2 + (nv) ** 2

@@ -1,0 +1,147 @@
+from contextlib import ExitStack
+
+import concourse.mybir as mybir
+
+K, T, S, N, V = 512, 1024, 512, 128, 256
+FLOPS = 2 * 2 * K * S * N
+
+F32 = mybir.dt.float32
+BF16 = mybir.dt.bfloat16
+I32 = mybir.dt.int32
+U32 = mybir.dt.uint32
+U16 = mybir.dt.uint16
+U8 = mybir.dt.uint8
+FP8X4 = mybir.dt.float8_e4m3fn_x4
+ACT = mybir.ActivationFunctionType
+ADD, SUB, MULT = mybir.AluOpType.add, mybir.AluOpType.subtract, mybir.AluOpType.mult
+
+P = 128
+PACK = 4
+PIECE = 256
+HALF = V // 2
+
+
+def tile_picked_yhorn_rob_p_kernel(tc, x_words, x_scales, w1, w2, gx, gy, gt, reg, offs, pos1, pos2, pos3, pos4, out):
+    nc = tc.nc
+    with ExitStack() as ctx:
+        lists = ctx.enter_context(tc.tile_pool(name="lists", bufs=1))
+        keep = ctx.enter_context(tc.tile_pool(name="keep", bufs=1))
+        psum = ctx.enter_context(tc.psum_pool(name="psum", bufs=1))
+
+        picked = lists.tile([P, S // 16], U16, name="picked")
+        nc.sync.dma_start(picked[:], offs)
+
+        table_scales = keep.tile([P, T], U8, name="table_scales", align_bytes=64)
+        nc.gpsimd.memset(table_scales[:].bitcast(I32), 0)
+        warm = keep.tile([P, 2], F32, name="warm")
+        nc.gpsimd.memset(warm[:, 0:1], 1.0)
+        nc.scalar.activation(warm[:, 1:2], warm[:, 0:1], ACT.Abs_reciprocal_sqrt)
+        for q in range(4):
+            nc.sync.dma_start(table_scales[32 * q : 32 * q + 4, :].bitcast(I32), x_scales[0, 4 * q : 4 * q + 4, :].bitcast(I32))
+        table_words = keep.tile([P, T], I32, name="table_words", align_bytes=64)
+        nc.sync.dma_start(table_words[:], x_words[0].rearrange("p n t -> p (n t)").bitcast(I32))
+
+        raw = []
+        for i, w in enumerate((w1, w2)):
+            w_raw = keep.tile([P, PACK, N], F32, name="w_raw%d" % i)
+            nc.sync.dma_start(w_raw[:], w.rearrange("(p j) m -> p j m", j=PACK))
+            raw.append(w_raw)
+
+        grad = keep.tile([P, 2, V], F32, name="grad")
+        nc.sync.dma_start(grad[:, 0, :], gx)
+        nc.sync.dma_start(grad[:, 1, :], gy)
+        reg_col = keep.tile([P, 1], F32, name="reg_col")
+        nc.sync.dma_start(reg_col[:], reg)
+        near = []
+        for i, pos in enumerate((pos1, pos2, pos3, pos4)):
+            pos_tile = lists.tile([P, V // 16], U16, name="near%d" % i)
+            nc.sync.dma_start(pos_tile[:], pos)
+            near.append(pos_tile)
+        gt_sb = keep.tile([P, V], F32, name="gt_sb")
+        nc.sync.dma_start(gt_sb[:], gt)
+
+        x_sc = keep.tile([P, S], U8, name="x_sc", align_bytes=64)
+        nc.vector.tensor_copy(x_sc[:], table_scales[:].indirect(picked[:]))
+
+        codes, planes = [], []
+        x_codes = []
+        for h in range(S // PIECE):
+            xc = keep.tile([P, PIECE], U32, name="x_codes%d" % h, align_bytes=64)
+            nc.vector.tensor_copy(xc[:], table_words[:].bitcast(U32).indirect(picked[:, h * PIECE // 16 : (h + 1) * PIECE // 16]))
+            x_codes.append(xc)
+            grouped = keep.tile([P, N, PACK], BF16, name="grouped%d" % h, align_bytes=64)
+            nc.scalar.copy(grouped[:], raw[h][:].rearrange("p j m -> p m j"))
+            wc = keep.tile([P, N], U32, name="w_codes%d" % h, align_bytes=64)
+            ws = keep.tile([P, N], U8, name="w_scales%d" % h, align_bytes=64)
+            nc.vector.quantize_mx(out=wc[:].bitcast(FP8X4), scales=ws[:], in_=grouped[:].rearrange("p m j -> p (m j)"))
+            codes.append(wc)
+            planes.append(ws)
+
+        flows = [keep.tile([P, S], F32, name="flow%d" % i) for i in range(2)]
+        for i in range(2):
+            for h in range(S // PIECE):
+                cols = slice(h * PIECE, (h + 1) * PIECE)
+                acc = psum.tile([P, PIECE], F32, name="acc%d%d" % (i, h))
+                nc.tensor.matmul_mx(out=acc[:], lhsT=codes[i][:].bitcast(FP8X4), lhsT_scale=planes[i][:],
+                                    rhs=x_codes[h][:].bitcast(FP8X4), rhs_scale=x_sc[:, cols], start=True, stop=True)
+                nc.scalar.activation(flows[i][:, cols], acc[:], ACT.Copy, scale=0.25)
+
+        grad_sq = keep.tile([P, 2, V], F32, name="grad_sq")
+        nc.scalar.activation(grad_sq[:], grad[:], ACT.Square)
+        norm_sq = keep.tile([P, V], F32, name="norm_sq")
+        nc.vector.tensor_tensor(norm_sq[:], grad_sq[:, 0, :], grad_sq[:, 1, :], ADD)
+        inv_root = keep.tile([P, V], F32, name="inv_root")
+        nc.scalar.activation(inv_root[:], norm_sq[:], ACT.Abs_reciprocal_sqrt, bias=reg_col[:])
+        inv_den = keep.tile([P, V], F32, name="inv_den")
+        nc.scalar.activation(inv_den[:], inv_root[:], ACT.Square)
+
+        mean = keep.tile([P, 2, V], F32, name="mean")
+        sums = [None, None]
+        for d in range(4):
+            for i in range(2):
+                window = flows[i][:].indirect(near[d][:])
+                if d == 3:
+                    target = mean[:, i, :]
+                else:
+                    part = keep.tile([P, V], F32, name="part%d%d" % (i, d))
+                    target = part[:]
+                if d == 0:
+                    nc.vector.tensor_copy(target, window)
+                else:
+                    nc.vector.tensor_tensor(target, window, sums[i], ADD)
+                sums[i] = target
+
+        pu = keep.tile([P, V], F32, name="pu")
+        nc.vector.tensor_tensor(pu[:], grad[:, 0, :], mean[:, 0, :], MULT)
+        pt = keep.tile([P, V], F32, name="pt")
+        nc.vector.tensor_tensor(pt[:], pu[:], gt_sb[:], ADD)
+
+        halves = [slice(h * HALF, (h + 1) * HALF) for h in range(2)]
+
+        def tiles(name, shape):
+            return [keep.tile(shape, F32, name="%s%d" % (name, h)) for h in range(2)]
+
+        pv, res, sq, rr, cc, step = [tiles(n, [P, HALF]) for n in ("pv", "res", "sq", "rr", "cc", "step")]
+        corr, new, new_sq = [tiles(n, [P, 2, HALF]) for n in ("corr", "new", "new_sq")]
+        result = tiles("result", [P, HALF])
+        for h, c in enumerate(halves):
+            nc.vector.tensor_tensor(pv[h][:], grad[:, 1, c], mean[:, 1, c], MULT)
+        for h, c in enumerate(halves):
+            nc.vector.tensor_tensor(res[h][:], pv[h][:], pt[:, c], ADD)
+        for h, c in enumerate(halves):
+            nc.scalar.activation(sq[h][:], res[h][:], ACT.Square)
+        for h, c in enumerate(halves):
+            nc.scalar.activation(rr[h][:], sq[h][:], ACT.Abs_reciprocal_sqrt, bias=0.2)
+        for h, c in enumerate(halves):
+            nc.vector.tensor_tensor(cc[h][:], res[h][:], inv_den[:, c], MULT)
+        for h, c in enumerate(halves):
+            nc.vector.tensor_tensor(step[h][:], cc[h][:], rr[h][:], MULT)
+        for h, c in enumerate(halves):
+            nc.vector.tensor_tensor(corr[h][:], grad[:, :, c], step[h][:].unsqueeze(1).to_broadcast([P, 2, HALF]), MULT)
+        for h, c in enumerate(halves):
+            nc.vector.tensor_tensor(new[h][:], mean[:, :, c], corr[h][:], SUB)
+        for h, c in enumerate(halves):
+            nc.scalar.activation(new_sq[h][:], new[h][:], ACT.Square)
+        for h, c in enumerate(halves):
+            nc.vector.tensor_tensor(result[h][:], new_sq[h][:, 0, :], new_sq[h][:, 1, :], ADD)
+            nc.sync.dma_start(out[:, c], result[h][:])

@@ -17,7 +17,8 @@ ADD, SUB, MULT = mybir.AluOpType.add, mybir.AluOpType.subtract, mybir.AluOpType.
 
 P = 128
 PACK = 4
-PIECE = 256
+U_PIECES = (slice(0, 256), slice(256, 384), slice(384, 512))
+V_PIECES = (slice(0, 256), slice(256, 512))
 HALF = V // 2
 
 
@@ -31,21 +32,18 @@ def tile_picked_yhorn_rob_p_kernel(tc, x_words, x_scales, w1, w2, gx, gy, gt, re
         picked = lists.tile([P, S // 16], U16, name="picked")
         nc.sync.dma_start(picked[:], offs)
 
-        table_scales = keep.tile([P, T], U8, name="table_scales", align_bytes=64)
+        raw = [keep.tile([P, PACK, N], F32, name="w_raw%d" % i) for i in range(2)]
+        nc.sync.dma_start(raw[0][:], w1.rearrange("(p j) m -> p j m", j=PACK))
+        table_scales = keep.tile([P, T], U8, name="table_scales", tag="scales0", align_bytes=64)
         nc.gpsimd.memset(table_scales[:].bitcast(I32), 0)
+        for q in range(4):
+            nc.sync.dma_start(table_scales[32 * q : 32 * q + 4, :].bitcast(I32), x_scales[0, 4 * q : 4 * q + 4, :].bitcast(I32))
         warm = keep.tile([P, 2], F32, name="warm")
         nc.gpsimd.memset(warm[:, 0:1], 1.0)
         nc.scalar.activation(warm[:, 1:2], warm[:, 0:1], ACT.Abs_reciprocal_sqrt)
-        for q in range(4):
-            nc.sync.dma_start(table_scales[32 * q : 32 * q + 4, :].bitcast(I32), x_scales[0, 4 * q : 4 * q + 4, :].bitcast(I32))
         table_words = keep.tile([P, T], I32, name="table_words", align_bytes=64)
         nc.sync.dma_start(table_words[:], x_words[0].rearrange("p n t -> p (n t)").bitcast(I32))
-
-        raw = []
-        for i, w in enumerate((w1, w2)):
-            w_raw = keep.tile([P, PACK, N], F32, name="w_raw%d" % i)
-            nc.sync.dma_start(w_raw[:], w.rearrange("(p j) m -> p j m", j=PACK))
-            raw.append(w_raw)
+        nc.sync.dma_start(raw[1][:], w2.rearrange("(p j) m -> p j m", j=PACK))
 
         grad = keep.tile([P, 2, V], F32, name="grad")
         nc.sync.dma_start(grad[:, 0, :], gx)
@@ -63,30 +61,33 @@ def tile_picked_yhorn_rob_p_kernel(tc, x_words, x_scales, w1, w2, gx, gy, gt, re
         x_sc = keep.tile([P, S], U8, name="x_sc", align_bytes=64)
         nc.vector.tensor_copy(x_sc[:], table_scales[:].indirect(picked[:]))
 
-        codes, planes = [], []
-        x_codes = []
-        for h in range(S // PIECE):
-            xc = keep.tile([P, PIECE], U32, name="x_codes%d" % h, align_bytes=64)
-            nc.vector.tensor_copy(xc[:], table_words[:].bitcast(U32).indirect(picked[:, h * PIECE // 16 : (h + 1) * PIECE // 16]))
-            x_codes.append(xc)
-            grouped = keep.tile([P, N, PACK], BF16, name="grouped%d" % h, align_bytes=64)
-            nc.scalar.copy(grouped[:], raw[h][:].rearrange("p j m -> p m j"))
-            wc = keep.tile([P, N], U32, name="w_codes%d" % h, align_bytes=64)
-            ws = keep.tile([P, N], U8, name="w_scales%d" % h, align_bytes=64)
-            nc.vector.quantize_mx(out=wc[:].bitcast(FP8X4), scales=ws[:], in_=grouped[:].rearrange("p m j -> p (m j)"))
-            codes.append(wc)
-            planes.append(ws)
+        def quantize(i):
+            grouped = keep.tile([P, N, PACK], BF16, name="grouped%d" % i, align_bytes=64)
+            nc.scalar.copy(grouped[:], raw[i][:].rearrange("p j m -> p m j"))
+            codes = keep.tile([P, N], U32, name="w_codes%d" % i, align_bytes=64)
+            plane = keep.tile([P, N], U8, name="w_scales%d" % i, tag="scales%d" % i, align_bytes=64)
+            nc.vector.quantize_mx(out=codes[:].bitcast(FP8X4), scales=plane[:], in_=grouped[:].rearrange("p m j -> p (m j)"))
+            return codes, plane
 
         flows = [keep.tile([P, S], F32, name="flow%d" % i) for i in range(2)]
-        for i in range(2):
-            for h in range(S // PIECE):
-                cols = slice(h * PIECE, (h + 1) * PIECE)
-                acc = psum.tile([P, PIECE], F32, name="acc%d%d" % (i, h))
-                nc.tensor.matmul_mx(out=acc[:], lhsT=codes[i][:].bitcast(FP8X4), lhsT_scale=planes[i][:],
-                                    rhs=x_codes[h][:].bitcast(FP8X4), rhs_scale=x_sc[:, cols], start=True, stop=True)
-                nc.scalar.activation(flows[i][:, cols], acc[:], ACT.Copy, scale=0.25)
 
-        grad_sq = keep.tile([P, 2, V], F32, name="grad_sq")
+        def product(i, weights, cols):
+            codes, plane = weights
+            acc = psum.tile([P, cols.stop - cols.start], F32, name="acc%d_%d" % (i, cols.start))
+            nc.tensor.matmul_mx(out=acc[:], lhsT=codes[:].bitcast(FP8X4), lhsT_scale=plane[:],
+                                rhs=x_codes[:, cols].bitcast(FP8X4), rhs_scale=x_sc[:, cols], start=True, stop=True)
+            nc.scalar.activation(flows[i][:, cols], acc[:], ACT.Copy, scale=0.25)
+
+        weights_u = quantize(0)
+        x_codes = keep.tile([P, S], U32, name="x_codes", tag="codes", align_bytes=64)
+        for cols in U_PIECES:
+            nc.vector.tensor_copy(x_codes[:, cols], table_words[:].bitcast(U32).indirect(picked[:, cols.start // 16 : cols.stop // 16]))
+            product(0, weights_u, cols)
+        weights_v = quantize(1)
+        for cols in V_PIECES:
+            product(1, weights_v, cols)
+
+        grad_sq = keep.tile([P, 2, V], F32, name="grad_sq", tag="codes", align_bytes=64)
         nc.scalar.activation(grad_sq[:], grad[:], ACT.Square)
         norm_sq = keep.tile([P, V], F32, name="norm_sq")
         nc.vector.tensor_tensor(norm_sq[:], grad_sq[:, 0, :], grad_sq[:, 1, :], ADD)
@@ -95,35 +96,37 @@ def tile_picked_yhorn_rob_p_kernel(tc, x_words, x_scales, w1, w2, gx, gy, gt, re
         inv_den = keep.tile([P, V], F32, name="inv_den")
         nc.scalar.activation(inv_den[:], inv_root[:], ACT.Square)
 
-        mean = keep.tile([P, 2, V], F32, name="mean")
-        sums = [None, None]
-        for d in range(4):
-            for i in range(2):
-                window = flows[i][:].indirect(near[d][:])
-                if d == 3:
-                    target = mean[:, i, :]
-                else:
-                    part = keep.tile([P, V], F32, name="part%d%d" % (i, d))
-                    target = part[:]
-                if d == 0:
-                    nc.vector.tensor_copy(target, window)
-                else:
-                    nc.vector.tensor_tensor(target, window, sums[i], ADD)
-                sums[i] = target
-
-        pu = keep.tile([P, V], F32, name="pu")
-        nc.vector.tensor_tensor(pu[:], grad[:, 0, :], mean[:, 0, :], MULT)
-        pt = keep.tile([P, V], F32, name="pt")
-        nc.vector.tensor_tensor(pt[:], pu[:], gt_sb[:], ADD)
-
         halves = [slice(h * HALF, (h + 1) * HALF) for h in range(2)]
 
         def tiles(name, shape):
             return [keep.tile(shape, F32, name="%s%d" % (name, h)) for h in range(2)]
 
-        pv, res, sq, rr, cc, step = [tiles(n, [P, HALF]) for n in ("pv", "res", "sq", "rr", "cc", "step")]
-        corr, new, new_sq = [tiles(n, [P, 2, HALF]) for n in ("corr", "new", "new_sq")]
+        sums = [None, None]
+        for d in range(3):
+            for i in range(2):
+                window = flows[i][:].indirect(near[d][:])
+                part = keep.tile([P, V], F32, name="part%d%d" % (i, d))
+                if d == 0:
+                    nc.vector.tensor_copy(part[:], window)
+                else:
+                    nc.vector.tensor_tensor(part[:], window, sums[i][:], ADD)
+                sums[i] = part
+        mean = keep.tile([P, 2, V], F32, name="mean")
+        nc.vector.tensor_tensor(mean[:, 0, :], flows[0][:].indirect(near[3][:]), sums[0][:], ADD)
+        pu = keep.tile([P, V], F32, name="pu")
+        pt = keep.tile([P, V], F32, name="pt")
+        nc.vector.tensor_tensor(mean[:, 1, halves[0]], flows[1][:].indirect(near[3][:, 0:8]), sums[1][:, halves[0]], ADD)
+        nc.vector.tensor_tensor(pu[:], grad[:, 0, :], mean[:, 0, :], MULT)
+        nc.vector.tensor_tensor(mean[:, 1, halves[1]], flows[1][:].indirect(near[3][:, 8:16]), sums[1][:, halves[1]], ADD)
+        nc.vector.tensor_tensor(pt[:], pu[:], gt_sb[:], ADD)
+
+        pv, res, sq, rr, cc = [tiles(n, [P, HALF]) for n in ("pv", "res", "sq", "rr", "cc")]
+        cg, corr, new, new_sq = [tiles(n, [P, 2, HALF]) for n in ("cg", "corr", "new", "new_sq")]
         result = tiles("result", [P, HALF])
+
+        def both(t):
+            return t[:].unsqueeze(1).to_broadcast([P, 2, HALF])
+
         for h, c in enumerate(halves):
             nc.vector.tensor_tensor(pv[h][:], grad[:, 1, c], mean[:, 1, c], MULT)
         for h, c in enumerate(halves):
@@ -135,13 +138,13 @@ def tile_picked_yhorn_rob_p_kernel(tc, x_words, x_scales, w1, w2, gx, gy, gt, re
         for h, c in enumerate(halves):
             nc.vector.tensor_tensor(cc[h][:], res[h][:], inv_den[:, c], MULT)
         for h, c in enumerate(halves):
-            nc.vector.tensor_tensor(step[h][:], cc[h][:], rr[h][:], MULT)
+            nc.vector.tensor_tensor(cg[h][:], grad[:, :, c], both(cc[h]), MULT)
         for h, c in enumerate(halves):
-            nc.vector.tensor_tensor(corr[h][:], grad[:, :, c], step[h][:].unsqueeze(1).to_broadcast([P, 2, HALF]), MULT)
+            nc.vector.tensor_tensor(corr[h][:], cg[h][:], both(rr[h]), MULT)
         for h, c in enumerate(halves):
-            nc.vector.tensor_tensor(new[h][:], mean[:, :, c], corr[h][:], SUB)
-        for h, c in enumerate(halves):
-            nc.scalar.activation(new_sq[h][:], new[h][:], ACT.Square)
+            for i in range(2):
+                nc.vector.tensor_tensor(new[h][:, i, :], mean[:, i, c], corr[h][:, i, :], SUB)
+                nc.scalar.activation(new_sq[h][:, i, :], new[h][:, i, :], ACT.Square)
         for h, c in enumerate(halves):
             nc.vector.tensor_tensor(result[h][:], new_sq[h][:, 0, :], new_sq[h][:, 1, :], ADD)
             nc.sync.dma_start(out[:, c], result[h][:])

@@ -1,6 +1,7 @@
 from contextlib import ExitStack
 
 import concourse.mybir as mybir
+from concourse.masks import make_identity
 
 K, T, S, N, V = 512, 1024, 512, 128, 256
 FLOPS = 2 * 2 * K * S * N
@@ -58,6 +59,9 @@ def tile_picked_yhorn_rob_p_kernel(tc, x_words, x_scales, w1, w2, gx, gy, gt, re
         gt_sb = keep.tile([P, V], F32, name="gt_sb")
         nc.sync.dma_start(gt_sb[:], gt)
 
+        identity = keep.tile([P, P], F32, name="identity")
+        make_identity(nc, identity[:])
+
         x_sc = keep.tile([P, S], U8, name="x_sc", align_bytes=64)
         nc.vector.tensor_copy(x_sc[:], table_scales[:].indirect(picked[:]))
 
@@ -71,35 +75,44 @@ def tile_picked_yhorn_rob_p_kernel(tc, x_words, x_scales, w1, w2, gx, gy, gt, re
 
         flows = [keep.tile([P, S], F32, name="flow%d" % i) for i in range(2)]
 
-        def product(i, weights, cols):
+        def product(i, weights, cols, bank):
             codes, plane = weights
-            acc = psum.tile([P, cols.stop - cols.start], F32, name="acc%d_%d" % (i, cols.start))
+            acc = psum.tile([P, cols.stop - cols.start], F32, name="acc", tag="bank%d" % bank)
             nc.tensor.matmul_mx(out=acc[:], lhsT=codes[:].bitcast(FP8X4), lhsT_scale=plane[:],
                                 rhs=x_codes[:, cols].bitcast(FP8X4), rhs_scale=x_sc[:, cols], start=True, stop=True)
             nc.scalar.activation(flows[i][:, cols], acc[:], ACT.Copy, scale=0.25)
 
         weights_u = quantize(0)
-        x_codes = keep.tile([P, S], U32, name="x_codes", tag="codes", align_bytes=64)
-        for cols in U_PIECES:
+        x_codes = keep.tile([P, S], U32, name="x_codes", align_bytes=64)
+        for n, cols in enumerate(U_PIECES):
             nc.vector.tensor_copy(x_codes[:, cols], table_words[:].bitcast(U32).indirect(picked[:, cols.start // 16 : cols.stop // 16]))
-            product(0, weights_u, cols)
+            product(0, weights_u, cols, n)
         weights_v = quantize(1)
-        for cols in V_PIECES:
-            product(1, weights_v, cols)
-
-        grad_sq = keep.tile([P, 2, V], F32, name="grad_sq", tag="codes", align_bytes=64)
-        nc.scalar.activation(grad_sq[:], grad[:], ACT.Square)
-        norm_sq = keep.tile([P, V], F32, name="norm_sq")
-        nc.vector.tensor_tensor(norm_sq[:], grad_sq[:, 0, :], grad_sq[:, 1, :], ADD)
-        inv_root = keep.tile([P, V], F32, name="inv_root")
-        nc.scalar.activation(inv_root[:], norm_sq[:], ACT.Abs_reciprocal_sqrt, bias=reg_col[:])
-        inv_den = keep.tile([P, V], F32, name="inv_den")
-        nc.scalar.activation(inv_den[:], inv_root[:], ACT.Square)
+        for n, cols in enumerate(V_PIECES):
+            product(1, weights_v, cols, 3 + n)
 
         halves = [slice(h * HALF, (h + 1) * HALF) for h in range(2)]
 
         def tiles(name, shape):
             return [keep.tile(shape, F32, name="%s%d" % (name, h)) for h in range(2)]
+
+        def turn_and_add(target, terms):
+            for n, term in enumerate(terms):
+                nc.tensor.matmul(target, term, identity[:], start=(n == 0), stop=(n == len(terms) - 1), is_transpose=True)
+
+        grad_t = psum.tile([P, 2, V], F32, name="grad_t", tag="bank4")
+        for i in range(2):
+            for c in halves:
+                turn_and_add(grad_t[:, i, c], [grad[:, i, c]])
+        grad_sq_t = keep.tile([P, 2, V], F32, name="grad_sq_t")
+        nc.scalar.activation(grad_sq_t[:], grad_t[:], ACT.Square)
+        norm_sq = psum.tile([P, V], F32, name="norm_sq", tag="bank6")
+        for c in halves:
+            turn_and_add(norm_sq[:, c], [grad_sq_t[:, 0, c], grad_sq_t[:, 1, c]])
+        inv_root = keep.tile([P, V], F32, name="inv_root", tag="sq0")
+        nc.scalar.activation(inv_root[:], norm_sq[:], ACT.Abs_reciprocal_sqrt, bias=reg_col[:])
+        inv_den = keep.tile([P, V], F32, name="inv_den")
+        nc.scalar.activation(inv_den[:], inv_root[:], ACT.Square)
 
         sums = [None, None]
         for d in range(3):

from contextlib import ExitStack

import concourse.mybir as mybir
from concourse.masks import make_identity

K, T, S, N, V = 512, 1024, 512, 128, 256
FLOPS = 2 * 2 * K * S * N

F32 = mybir.dt.float32
BF16 = mybir.dt.bfloat16
I32 = mybir.dt.int32
U32 = mybir.dt.uint32
U16 = mybir.dt.uint16
U8 = mybir.dt.uint8
FP8X4 = mybir.dt.float8_e4m3fn_x4
ACT = mybir.ActivationFunctionType
ADD, SUB, MULT = mybir.AluOpType.add, mybir.AluOpType.subtract, mybir.AluOpType.mult

P = 128
PACK = 4
U_PIECES = (slice(0, 256), slice(256, 384), slice(384, 512))
V_PIECES = (slice(0, 256), slice(256, 512))
HALF = V // 2


def tile_picked_yhorn_rob_p_kernel(tc, x_words, x_scales, w1, w2, gx, gy, gt, reg, offs, pos1, pos2, pos3, pos4, out):
    nc = tc.nc
    with ExitStack() as ctx:
        lists = ctx.enter_context(tc.tile_pool(name="lists", bufs=1))
        keep = ctx.enter_context(tc.tile_pool(name="keep", bufs=1))
        psum = ctx.enter_context(tc.psum_pool(name="psum", bufs=1))

        picked = lists.tile([P, S // 16], U16, name="picked")
        nc.sync.dma_start(picked[:], offs)

        raw = [keep.tile([P, PACK, N], F32, name="w_raw%d" % i) for i in range(2)]
        nc.sync.dma_start(raw[0][:], w1.rearrange("(p j) m -> p j m", j=PACK))
        table_scales = keep.tile([P, T], U8, name="table_scales", tag="scales0", align_bytes=64)
        nc.gpsimd.memset(table_scales[:].bitcast(I32), 0)
        for q in range(4):
            nc.sync.dma_start(table_scales[32 * q : 32 * q + 4, :].bitcast(I32), x_scales[0, 4 * q : 4 * q + 4, :].bitcast(I32))
        warm = keep.tile([P, 2], F32, name="warm")
        nc.gpsimd.memset(warm[:, 0:1], 1.0)
        nc.scalar.activation(warm[:, 1:2], warm[:, 0:1], ACT.Abs_reciprocal_sqrt)
        table_words = keep.tile([P, T], I32, name="table_words", align_bytes=64)
        nc.sync.dma_start(table_words[:], x_words[0].rearrange("p n t -> p (n t)").bitcast(I32))
        nc.sync.dma_start(raw[1][:], w2.rearrange("(p j) m -> p j m", j=PACK))

        grad = keep.tile([P, 2, V], F32, name="grad")
        nc.sync.dma_start(grad[:, 0, :], gx)
        nc.sync.dma_start(grad[:, 1, :], gy)
        reg_col = keep.tile([P, 1], F32, name="reg_col")
        nc.sync.dma_start(reg_col[:], reg)
        near = []
        for i, pos in enumerate((pos1, pos2, pos3, pos4)):
            pos_tile = lists.tile([P, V // 16], U16, name="near%d" % i)
            nc.sync.dma_start(pos_tile[:], pos)
            near.append(pos_tile)
        gt_sb = keep.tile([P, V], F32, name="gt_sb")
        nc.sync.dma_start(gt_sb[:], gt)

        identity = keep.tile([P, P], F32, name="identity")
        make_identity(nc, identity[:])

        x_sc = keep.tile([P, S], U8, name="x_sc", align_bytes=64)
        nc.vector.tensor_copy(x_sc[:], table_scales[:].indirect(picked[:]))

        def quantize(i):
            grouped = keep.tile([P, N, PACK], BF16, name="grouped%d" % i, align_bytes=64)
            nc.scalar.copy(grouped[:], raw[i][:].rearrange("p j m -> p m j"))
            codes = keep.tile([P, N], U32, name="w_codes%d" % i, align_bytes=64)
            plane = keep.tile([P, N], U8, name="w_scales%d" % i, tag="scales%d" % i, align_bytes=64)
            nc.vector.quantize_mx(out=codes[:].bitcast(FP8X4), scales=plane[:], in_=grouped[:].rearrange("p m j -> p (m j)"))
            return codes, plane

        flows = [keep.tile([P, S], F32, name="flow%d" % i) for i in range(2)]

        def product(i, weights, cols, bank):
            codes, plane = weights
            acc = psum.tile([P, cols.stop - cols.start], F32, name="acc", tag="bank%d" % bank)
            nc.tensor.matmul_mx(out=acc[:], lhsT=codes[:].bitcast(FP8X4), lhsT_scale=plane[:],
                                rhs=x_codes[:, cols].bitcast(FP8X4), rhs_scale=x_sc[:, cols], start=True, stop=True)
            nc.scalar.activation(flows[i][:, cols], acc[:], ACT.Copy, scale=0.25)

        weights_u = quantize(0)
        x_codes = keep.tile([P, S], U32, name="x_codes", align_bytes=64)
        for n, cols in enumerate(U_PIECES):
            nc.vector.tensor_copy(x_codes[:, cols], table_words[:].bitcast(U32).indirect(picked[:, cols.start // 16 : cols.stop // 16]))
            product(0, weights_u, cols, n)
        weights_v = quantize(1)
        for n, cols in enumerate(V_PIECES):
            product(1, weights_v, cols, 3 + n)

        halves = [slice(h * HALF, (h + 1) * HALF) for h in range(2)]

        def tiles(name, shape):
            return [keep.tile(shape, F32, name="%s%d" % (name, h)) for h in range(2)]

        def turn_and_add(target, terms):
            for n, term in enumerate(terms):
                nc.tensor.matmul(target, term, identity[:], start=(n == 0), stop=(n == len(terms) - 1), is_transpose=True)

        grad_t = psum.tile([P, 2, V], F32, name="grad_t", tag="bank4")
        for i in range(2):
            for c in halves:
                turn_and_add(grad_t[:, i, c], [grad[:, i, c]])
        grad_sq_t = keep.tile([P, 2, V], F32, name="grad_sq_t")
        nc.scalar.activation(grad_sq_t[:], grad_t[:], ACT.Square)
        norm_sq = psum.tile([P, V], F32, name="norm_sq", tag="bank6")
        for c in halves:
            turn_and_add(norm_sq[:, c], [grad_sq_t[:, 0, c], grad_sq_t[:, 1, c]])
        inv_root = keep.tile([P, V], F32, name="inv_root", tag="sq0")
        nc.scalar.activation(inv_root[:], norm_sq[:], ACT.Abs_reciprocal_sqrt, bias=reg_col[:])
        inv_den = keep.tile([P, V], F32, name="inv_den")
        nc.scalar.activation(inv_den[:], inv_root[:], ACT.Square)

        sums = [None, None]
        for d in range(3):
            for i in range(2):
                window = flows[i][:].indirect(near[d][:])
                part = keep.tile([P, V], F32, name="part%d%d" % (i, d))
                if d == 0:
                    nc.vector.tensor_copy(part[:], window)
                else:
                    nc.vector.tensor_tensor(part[:], window, sums[i][:], ADD)
                sums[i] = part
        mean = keep.tile([P, 2, V], F32, name="mean")
        nc.vector.tensor_tensor(mean[:, 0, :], flows[0][:].indirect(near[3][:]), sums[0][:], ADD)
        pu = keep.tile([P, V], F32, name="pu")
        pt = keep.tile([P, V], F32, name="pt")
        nc.vector.tensor_tensor(mean[:, 1, halves[0]], flows[1][:].indirect(near[3][:, 0:8]), sums[1][:, halves[0]], ADD)
        nc.vector.tensor_tensor(pu[:], grad[:, 0, :], mean[:, 0, :], MULT)
        nc.vector.tensor_tensor(mean[:, 1, halves[1]], flows[1][:].indirect(near[3][:, 8:16]), sums[1][:, halves[1]], ADD)
        nc.vector.tensor_tensor(pt[:], pu[:], gt_sb[:], ADD)

        pv, res, sq, rr, cc = [tiles(n, [P, HALF]) for n in ("pv", "res", "sq", "rr", "cc")]
        cg, corr, new, new_sq = [tiles(n, [P, 2, HALF]) for n in ("cg", "corr", "new", "new_sq")]
        result = tiles("result", [P, HALF])

        def both(t):
            return t[:].unsqueeze(1).to_broadcast([P, 2, HALF])

        for h, c in enumerate(halves):
            nc.vector.tensor_tensor(pv[h][:], grad[:, 1, c], mean[:, 1, c], MULT)
        for h, c in enumerate(halves):
            nc.vector.tensor_tensor(res[h][:], pv[h][:], pt[:, c], ADD)
        for h, c in enumerate(halves):
            nc.scalar.activation(sq[h][:], res[h][:], ACT.Square)
        for h, c in enumerate(halves):
            nc.scalar.activation(rr[h][:], sq[h][:], ACT.Abs_reciprocal_sqrt, bias=0.2)
        for h, c in enumerate(halves):
            nc.vector.tensor_tensor(cc[h][:], res[h][:], inv_den[:, c], MULT)
        for h, c in enumerate(halves):
            nc.vector.tensor_tensor(cg[h][:], grad[:, :, c], both(cc[h]), MULT)
        for h, c in enumerate(halves):
            nc.vector.tensor_tensor(corr[h][:], cg[h][:], both(rr[h]), MULT)
        for h, c in enumerate(halves):
            for i in range(2):
                nc.vector.tensor_tensor(new[h][:, i, :], mean[:, i, c], corr[h][:, i, :], SUB)
                nc.scalar.activation(new_sq[h][:, i, :], new[h][:, i, :], ACT.Square)
        for h, c in enumerate(halves):
            nc.vector.tensor_tensor(result[h][:], new_sq[h][:, 0, :], new_sq[h][:, 1, :], ADD)
            nc.sync.dma_start(out[:, c], result[h][:])
